import numpy as np
import ml_dtypes


def mxq(x, axis, fmt="e4m3"):
    dtype, down = {"e4m3": (ml_dtypes.float8_e4m3fn, 7), "e5m2": (ml_dtypes.float8_e5m2, 14)}[fmt]
    v = np.moveaxis(np.asarray(x, np.float32).astype(ml_dtypes.bfloat16).astype(np.float64), axis, -1)
    blocks = v.reshape(v.shape[:-1] + (-1, 32))
    amax = np.abs(blocks).max(-1, keepdims=True)
    byte = np.maximum(np.where(amax > 0, np.frexp(amax)[1] - 1 + 127, 0) - down, 1)
    scale = np.exp2(byte - 127.0)
    codes = (blocks / scale).astype(np.float32).astype(dtype).astype(np.float64)
    return np.moveaxis((codes * scale).reshape(v.shape), -1, axis)


WIDE = False


def mx_kscale(k):
    if not WIDE:
        return np.ones(k)
    levels = np.array([10, -10, 5, -5, 0])
    if k % 512:
        return np.exp2(np.random.permutation(np.resize(levels, k // 32))).repeat(32)
    a = np.empty((k // 512, 16))
    for p in range(k // 512):
        a[p, :8] = np.random.permutation(np.resize(levels, 8))
        for g in range(8):
            far = levels[np.abs(levels - a[p, g]) >= 10]
            a[p, g + 8] = far[np.random.randint(len(far))]
    return np.exp2(a.ravel()).repeat(32)


def f64(x):
    return np.asarray(x).astype(np.float64)


def striped(idx):
    return np.tile(idx.reshape(-1, 16).T, (8, 1)).astype(np.uint16)


def unstriped(offs):
    return offs[:16].T.reshape(-1).astype(np.int64)


def striped8(idx):
    return np.concatenate([x.reshape(-1, 16).T for x in idx]).astype(np.uint16)


def runs(offs, k):
    lists = np.stack([offs[16 * r : 16 * r + 16].T.reshape(-1) for r in range(8)]).astype(np.int64)
    return lists[np.arange(k) % 512 // 64]


def pack_weight(w):
    k, n = w.shape
    w = f64(np.asarray(w, np.float32).astype(ml_dtypes.bfloat16)).reshape(k // 32, 32, n)
    amax = np.abs(w).max(1)
    byte = np.clip(np.where(amax > 0, np.frexp(amax)[1] - 1 + 127 - 7, 1), 1, 254)
    scaled = (w * np.exp2(127.0 - byte)[:, None, :]).reshape(k, n).astype(np.float32)
    words = np.ascontiguousarray(scaled.reshape(k // 512, 128, 4, n).transpose(0, 1, 3, 2)).astype(ml_dtypes.float8_e4m3fn).view(np.uint8)
    return words, np.ascontiguousarray(byte.astype(np.uint8).reshape(k // 512, 16, n))


def unpack_weight(words, scales):
    g, p, n, _ = words.shape
    vals = np.ascontiguousarray(words).view(ml_dtypes.float8_e4m3fn).astype(np.float64) * np.repeat(np.exp2(scales.astype(np.float64) - 127.0), 8, axis=1)[..., None]
    return vals.transpose(0, 1, 3, 2).reshape(g * 512, n)


def relu(v):
    return np.maximum(v, 0.0)


def sigmoid(v):
    return 1.0 / (1.0 + np.exp(-np.maximum(v, -700.0)))

def planes(y):
    n, m = y.shape
    v = y.astype(np.float32).astype(ml_dtypes.bfloat16).astype(np.float64).reshape(n // 32, 32, m)
    top = np.abs(v).max(1)
    byte = np.clip(np.where(top > 0, np.frexp(top)[1] - 1 + 127 - 7, 1), 1, 254)
    codes = (v * np.exp2(127.0 - byte)[:, None, :]).reshape(n, m).astype(np.float32).astype(ml_dtypes.float8_e4m3fn).view(np.uint8)
    words = codes.reshape(n // 512, 128, 4, m).transpose(0, 1, 3, 2)
    return np.ascontiguousarray(words), np.ascontiguousarray(byte.astype(np.uint8).reshape(n // 512, 16, m))


K, T, S, G, H, C, W = 512, 1024, 512, 2048, 512, 512, 256


def setup_inputs():
    n = np.random.standard_normal
    s = mx_kscale(K)[:, None]
    packed_xT = pack_weight(n((K, T)) * s)
    packed_dT = pack_weight(n((K, G)) / s)
    perm = np.stack([np.random.permutation(S) for _ in range(8)])
    return {
        "x_words": packed_xT[0],
        "x_scales": packed_xT[1],
        "d_words": packed_dT[0],
        "d_scales": packed_dT[1],
        "gs": (np.random.uniform(0.5, 1.5, (K, 1)) / s).astype(np.float32),
        "offs": striped(np.random.permutation(T)[:S]),
        "k1": striped8(np.random.randint(0, G, (8, H))),
        "n1": striped8(np.stack([np.random.permutation(S) for _ in range(8)])),
        "n2": striped8(np.stack([np.random.permutation(S) for _ in range(8)])),
        "cand": striped(np.random.permutation(T)[:C]),
        "n3": striped8(perm[:, :W]),
        "n4": striped8(perm[:, W:]),
    }


def reference(x_words, x_scales, d_words, d_scales, gs, offs, k1, n1, n2, cand, n3, n4):
    x_cand = unpack_weight(x_words, x_scales)[:, unstriped(cand)]
    d_k1 = unpack_weight(d_words, d_scales)[np.arange(K)[:, None], runs(k1, K)]
    xq = unpack_weight(x_words, x_scales)[:, unstriped(offs)]
    h = 0.0625 * (d_k1.T @ xq)
    pa = h - (h[np.arange(H)[:, None], runs(n1, H)])
    pb = h[np.arange(H)[:, None], runs(n2, H)] - h
    z = f64(gs) * (relu(np.minimum(pa, pb)) - (relu(-1.0 * np.maximum(pa, pb))))
    s = 0.0625 * ((x_cand.T @ mxq(z, 0, "e4m3")))
    pa2 = s[np.arange(C)[:, None], runs(n3, C)]
    pb2 = s[np.arange(C)[:, None], runs(n4, C)]
    ra = pa2 * sigmoid(pb2)
    out = s.copy()
    out[np.arange(C)[:, None], runs(n4, C)] = ra
    return (out,) + planes(out)

@@ -1,0 +1,210 @@
+from contextlib import ExitStack
+
+import concourse.mybir as mybir
+
+K, T, S, G, H, C, W = 512, 1024, 512, 2048, 512, 512, 256
+FLOPS = 2 * K * H * S + 2 * K * C * S
+
+F32 = mybir.dt.float32
+BF16 = mybir.dt.bfloat16
+I32 = mybir.dt.int32
+U32 = mybir.dt.uint32
+U16 = mybir.dt.uint16
+U8 = mybir.dt.uint8
+FP8X4 = mybir.dt.float8_e4m3fn_x4
+ALU = mybir.AluOpType
+ACT = mybir.ActivationFunctionType
+
+P = 128
+PACK = 4
+CHUNKS = ((0, 256), (256, 384), (384, 512))
+HALVES = ((0, 256), (256, 512))
+
+
+def tile_picked_pqcminmodfold_none_po_kernel(
+    tc, x_words, x_scales, d_words, d_scales, gs, offs, k1, n1, n2, cand, n3, n4, out_0, out_1, out_2
+):
+    nc = tc.nc
+    with ExitStack() as ctx:
+        sb = ctx.enter_context(tc.tile_pool(name="sb", bufs=1))
+        ps = ctx.enter_context(tc.psum_pool(name="ps", bufs=1))
+
+        def new(name, shape, dtype):
+            return sb.tile(shape, dtype, name=name, align_bytes=64)
+
+        def load_list(name, source):
+            tile = new(name, [P, source.shape[1]], U16)
+            nc.sync.dma_start(tile[:], source)
+            return tile
+
+        def words_of(source):
+            return source[0].rearrange("p n t -> p (n t)").bitcast(I32)
+
+        d_scale_win = new("d_scale_win", [P, G], U8)
+        x_scale_win = new("x_scale_win", [P, T], U8)
+        nc.vector.memset(d_scale_win[:].bitcast(I32), 0)
+        nc.vector.memset(x_scale_win[:].bitcast(I32), 0)
+        nc.scalar.dma_start(d_scale_win[0:P:8, :].bitcast(I32), d_scales[0].bitcast(I32))
+        for q in range(4):
+            nc.scalar.dma_start(
+                x_scale_win[32 * q : 32 * q + 4, :].bitcast(I32), x_scales[0][4 * q : 4 * q + 4, :].bitcast(I32)
+            )
+
+        offs_t = load_list("offs_t", offs)
+        x_word_win = new("x_word_win", [P, T], U32)
+        nc.sync.dma_start(x_word_win[:].bitcast(I32), words_of(x_words))
+        k1_t = load_list("k1_t", k1)
+        d_word_win = new("d_word_win", [P, G], U32)
+        nc.sync.dma_start(d_word_win[:].bitcast(I32), words_of(d_words))
+        cand_t = load_list("cand_t", cand)
+        gs_t = new("gs_t", [P, PACK], F32)
+        nc.sync.dma_start(gs_t[:], gs.rearrange("(p t) o -> p (t o)", t=PACK))
+        n1_t = load_list("n1_t", n1)
+        n2_t = load_list("n2_t", n2)
+        n3_t = load_list("n3_t", n3)
+        n4_t = load_list("n4_t", n4)
+
+        warm = new("warm", [P, PACK], F32)
+        nc.scalar.activation(warm[:], gs_t[:], ACT.Sigmoid)
+        g_pos = new("g_pos", [P, PACK], F32)
+        g_neg = new("g_neg", [P, PACK], F32)
+        nc.scalar.mul(g_pos[:], gs_t[:], 0.0625)
+        nc.scalar.mul(g_neg[:], gs_t[:], -0.0625)
+
+        def gather(name, window, offsets, dtype):
+            picked = new(name, [P, 512], dtype)
+            nc.vector.tensor_copy(picked[:], window[:].indirect(offsets[:]))
+            return picked
+
+        def deal(name, picked, dtype, view):
+            dealt = new(name, [P, 512], dtype)
+            nc.vector.tensor_copy(
+                dealt[:].bitcast(view).rearrange("p (t m) -> p m t", t=PACK),
+                picked[:].bitcast(view).rearrange("p (m t) -> p m t", t=PACK),
+            )
+            return dealt
+
+        xq_w = gather("xq_w", x_word_win, offs_t, U32)
+        d_sc = deal("d_sc", gather("d_sc_raw", d_scale_win, k1_t, U8), U8, U8)
+        for r in range(1, 4):
+            nc.sync.dma_start(d_sc[r:P:32, :].bitcast(I32), d_sc[8 * r : P : 32, :].bitcast(I32))
+        d_w = deal("d_w", gather("d_w_raw", d_word_win, k1_t, U32), U32, I32)
+        xq_sc = gather("xq_sc", x_scale_win, offs_t, U8)
+
+        h_pos, h_neg = [], []
+        for t in range(PACK):
+            cols = slice(P * t, P * (t + 1))
+            acc = ps.tile([P, S], F32, name=f"h_acc{t}")
+            nc.tensor.matmul_mx(
+                out=acc[:], lhsT=d_w[:, cols].bitcast(FP8X4), lhsT_scale=d_sc[:, cols],
+                rhs=xq_w[:].bitcast(FP8X4), rhs_scale=xq_sc[:], start=True, stop=True,
+            )
+            pos = new(f"h_pos{t}", [P, S], F32)
+            neg = new(f"h_neg{t}", [P, S], F32)
+            nc.scalar.activation(pos[:], acc[:], ACT.Copy, scale=g_pos[:, t : t + 1])
+            nc.scalar.activation(neg[:], acc[:], ACT.Copy, scale=g_neg[:, t : t + 1])
+            h_pos.append(pos)
+            h_neg.append(neg)
+
+        c_w = deal("c_w", gather("c_w_raw", x_word_win, cand_t, U32), U32, I32)
+        c_sc = deal("c_sc", gather("c_sc_raw", x_scale_win, cand_t, U8), U8, U8)
+
+        s_acc = [ps.tile([P, S], F32, name=f"s_acc{t}") for t in range(PACK)]
+        s_t = [new(f"s_t{t}", [P, S], F32) for t in range(PACK)]
+
+        def weave(name, planes, n):
+            woven = new(name, [P, n, PACK], BF16)
+            nc.scalar.copy(
+                woven[:].rearrange("p (c i) t -> p c t i", i=4),
+                planes[:].rearrange("p t (c i) -> p c t i", i=4),
+            )
+            return woven[:].rearrange("p n t -> p (n t)")
+
+        def differences(c):
+            lo, hi = CHUNKS[c]
+            n = hi - lo
+            lists = slice(lo // 16, hi // 16)
+            pa = new(f"pa{c}", [P, PACK, n], F32)
+            pb = new(f"pb{c}", [P, PACK, n], F32)
+
+            def pa_plane(t):
+                nc.vector.tensor_tensor(pa[:, t, :], h_neg[t][:].indirect(n1_t[:, lists]), h_pos[t][:, lo:hi], ALU.add)
+
+            def pb_plane(t):
+                nc.vector.tensor_tensor(pb[:, t, :], h_pos[t][:].indirect(n2_t[:, lists]), h_neg[t][:, lo:hi], ALU.add)
+
+            if c == 0:
+                for t in range(PACK):
+                    pb_plane(t)
+                    pa_plane(t)
+            else:
+                for t in range(PACK):
+                    pb_plane(t)
+                for t in range(PACK):
+                    pa_plane(t)
+            pb16 = weave(f"pb16_{c}", pb, n)
+            pa16 = weave(f"pa16_{c}", pa, n)
+            return pa16, pb16
+
+        def scores(c, pa16, pb16):
+            lo, hi = CHUNKS[c]
+            n = hi - lo
+            below = new(f"below{c}", [P, PACK * n], BF16)
+            above = new(f"above{c}", [P, PACK * n], BF16)
+            raised = new(f"raised{c}", [P, PACK * n], BF16)
+            z16 = new(f"z16_{c}", [P, PACK * n], BF16)
+            nc.vector.tensor_scalar_min(below[:], pb16, 0.0)
+            nc.vector.tensor_scalar_max(above[:], pb16, 0.0)
+            nc.vector.tensor_tensor(raised[:], pa16, below[:], ALU.max)
+            nc.vector.tensor_tensor(z16[:], raised[:], above[:], ALU.min)
+            z_w = new(f"z_w{c}", [P, n], U32)
+            z_sc = new(f"z_sc{c}", [P, n], U8)
+            nc.vector.quantize_mx(out=z_w[:].bitcast(FP8X4), scales=z_sc[:], in_=z16[:])
+            for t in range(PACK):
+                cols = slice(P * t, P * (t + 1))
+                nc.tensor.matmul_mx(
+                    out=s_acc[t][:, lo:hi], lhsT=c_w[:, cols].bitcast(FP8X4), lhsT_scale=c_sc[:, cols],
+                    rhs=z_w[:].bitcast(FP8X4), rhs_scale=z_sc[:], start=True, stop=True,
+                )
+                nc.scalar.mul(s_t[t][:, lo:hi], s_acc[t][:, lo:hi], 0.0625)
+
+        pending = differences(0)
+        for c in range(1, len(CHUNKS)):
+            ahead = differences(c)
+            scores(c - 1, *pending)
+            pending = ahead
+        scores(len(CHUNKS) - 1, *pending)
+
+        out_rows = out_0.rearrange("(p t) j -> t p j", t=PACK)
+        woven = new("woven", [P, S, PACK], BF16)
+        gates = []
+        for t in range(PACK):
+            gate = new(f"gate{t}", [P, W], F32)
+            nc.scalar.activation(gate[:], s_t[t][:].indirect(n4_t[:]), ACT.Sigmoid)
+            gates.append(gate)
+        for t in range(PACK):
+            pa2 = new(f"pa2_{t}", [P, W], F32)
+            nc.vector.tensor_copy(pa2[:], s_t[t][:].indirect(n3_t[:]))
+            nc.vector.tensor_tensor(s_t[t][:].indirect(n4_t[:]), pa2[:], gates[t][:], ALU.mult)
+            nc.sync.dma_start(out_rows[t], s_t[t][:])
+            if t < 2:
+                nc.scalar.copy(woven[:, :, t], s_t[t][:])
+            elif t == 2:
+                nc.scalar.copy(woven[:, :, 2:4], s_t[t][:].unsqueeze(2).to_broadcast([P, S, 2]))
+            else:
+                for lo, hi in HALVES:
+                    nc.vector.tensor_copy(woven[:, lo:hi, t], s_t[t][:, lo:hi])
+
+        o_w = new("o_w", [P, S], U32)
+        o_sc = new("o_sc", [P, S], U8)
+        for lo, hi in HALVES:
+            nc.vector.quantize_mx(
+                out=o_w[:, lo:hi].bitcast(FP8X4), scales=o_sc[:, lo:hi],
+                in_=woven[:, lo:hi, :].rearrange("p n t -> p (n t)"),
+            )
+            nc.sync.dma_start(words_of(out_1)[:, lo:hi], o_w[:, lo:hi].bitcast(I32))
+        for q in range(4):
+            engine = nc.scalar if q % 2 else nc.sync
+            engine.dma_start(
+                out_2[0][4 * q : 4 * q + 4, :].bitcast(I32), o_sc[32 * q : 32 * q + 4, :].bitcast(I32)
+            )

@@ -17,7 +17,6 @@ ACT = mybir.ActivationFunctionType
 
 P = 128
 PACK = 4
-CHUNKS = ((0, 256), (256, 384), (384, 512))
 HALVES = ((0, 256), (256, 512))
 
 
@@ -29,8 +28,8 @@ def tile_picked_pqcminmodfold_none_po_kernel(
         sb = ctx.enter_context(tc.tile_pool(name="sb", bufs=1))
         ps = ctx.enter_context(tc.psum_pool(name="ps", bufs=1))
 
-        def new(name, shape, dtype):
-            return sb.tile(shape, dtype, name=name, align_bytes=64)
+        def new(name, shape, dtype, tag=None):
+            return sb.tile(shape, dtype, name=name, tag=tag or name, align_bytes=64)
 
         def load_list(name, source):
             tile = new(name, [P, source.shape[1]], U16)
@@ -42,18 +41,19 @@ def tile_picked_pqcminmodfold_none_po_kernel(
 
         d_scale_win = new("d_scale_win", [P, G], U8)
         x_scale_win = new("x_scale_win", [P, T], U8)
-        nc.vector.memset(d_scale_win[:].bitcast(I32), 0)
         nc.vector.memset(x_scale_win[:].bitcast(I32), 0)
-        nc.scalar.dma_start(d_scale_win[0:P:8, :].bitcast(I32), d_scales[0].bitcast(I32))
         for q in range(4):
             nc.scalar.dma_start(
                 x_scale_win[32 * q : 32 * q + 4, :].bitcast(I32), x_scales[0][4 * q : 4 * q + 4, :].bitcast(I32)
             )
 
+        k1_t = load_list("k1_t", k1)
+        nc.sync.dma_start(
+            d_scale_win[:].bitcast(I32), d_scales[0].bitcast(I32).unsqueeze(1).to_broadcast([16, 8, G // 4])
+        )
         offs_t = load_list("offs_t", offs)
         x_word_win = new("x_word_win", [P, T], U32)
         nc.sync.dma_start(x_word_win[:].bitcast(I32), words_of(x_words))
-        k1_t = load_list("k1_t", k1)
         d_word_win = new("d_word_win", [P, G], U32)
         nc.sync.dma_start(d_word_win[:].bitcast(I32), words_of(d_words))
         cand_t = load_list("cand_t", cand)
@@ -66,134 +66,180 @@ def tile_picked_pqcminmodfold_none_po_kernel(
 
         warm = new("warm", [P, PACK], F32)
         nc.scalar.activation(warm[:], gs_t[:], ACT.Sigmoid)
-        g_pos = new("g_pos", [P, PACK], F32)
-        g_neg = new("g_neg", [P, PACK], F32)
-        nc.scalar.mul(g_pos[:], gs_t[:], 0.0625)
-        nc.scalar.mul(g_neg[:], gs_t[:], -0.0625)
+        gains = new("gains", [P, 2, PACK], F32)
+        nc.scalar.mul(gains[:, 0, :], gs_t[:], 0.0625)
+        nc.scalar.mul(gains[:, 1, :], gs_t[:], -0.0625)
 
-        def gather(name, window, offsets, dtype):
-            picked = new(name, [P, 512], dtype)
+        def gather(name, window, offsets, dtype, tag=None):
+            picked = new(name, [P, 512], dtype, tag)
             nc.vector.tensor_copy(picked[:], window[:].indirect(offsets[:]))
             return picked
 
-        def deal(name, picked, dtype, view):
-            dealt = new(name, [P, 512], dtype)
+        def deal(name, picked, dtype, view, t0=0, t1=PACK, tag=None):
+            dealt = new(name, [P, P * (t1 - t0)], dtype, tag)
+            run = 4 if dtype == U32 else 16
             nc.vector.tensor_copy(
-                dealt[:].bitcast(view).rearrange("p (t m) -> p m t", t=PACK),
-                picked[:].bitcast(view).rearrange("p (m t) -> p m t", t=PACK),
+                dealt[:].bitcast(view).rearrange("p (t c i) -> p c t i", i=run, c=P // run),
+                picked[:].bitcast(view).rearrange("p (c i t) -> p c t i", i=run, t=PACK)[:, :, t0:t1, :],
             )
             return dealt
 
+        d_sc_raw = gather("d_sc_raw", d_scale_win, k1_t, U8)
         xq_w = gather("xq_w", x_word_win, offs_t, U32)
-        d_sc = deal("d_sc", gather("d_sc_raw", d_scale_win, k1_t, U8), U8, U8)
+        d_sc = deal("d_sc", d_sc_raw, U8, U8)
         for r in range(1, 4):
             nc.sync.dma_start(d_sc[r:P:32, :].bitcast(I32), d_sc[8 * r : P : 32, :].bitcast(I32))
-        d_w = deal("d_w", gather("d_w_raw", d_word_win, k1_t, U32), U32, I32)
         xq_sc = gather("xq_sc", x_scale_win, offs_t, U8)
+        d_w_raw = gather("d_w_raw", d_word_win, k1_t, U32)
+        c_sc_raw = gather("c_sc_raw", x_scale_win, cand_t, U8, "d_word_win")
+        d_w = deal("d_w", d_w_raw, U32, I32)
 
         h_pos, h_neg = [], []
         for t in range(PACK):
             cols = slice(P * t, P * (t + 1))
-            acc = ps.tile([P, S], F32, name=f"h_acc{t}")
+            acc = ps.tile([P, S], F32, name=f"h_acc{t}", tag=f"h_acc{t}")
             nc.tensor.matmul_mx(
                 out=acc[:], lhsT=d_w[:, cols].bitcast(FP8X4), lhsT_scale=d_sc[:, cols],
                 rhs=xq_w[:].bitcast(FP8X4), rhs_scale=xq_sc[:], start=True, stop=True,
             )
             pos = new(f"h_pos{t}", [P, S], F32)
             neg = new(f"h_neg{t}", [P, S], F32)
-            nc.scalar.activation(pos[:], acc[:], ACT.Copy, scale=g_pos[:, t : t + 1])
-            nc.scalar.activation(neg[:], acc[:], ACT.Copy, scale=g_neg[:, t : t + 1])
+            nc.scalar.activation(pos[:], acc[:], ACT.Copy, scale=gains[:, 0, t : t + 1])
+            nc.scalar.activation(neg[:], acc[:], ACT.Copy, scale=gains[:, 1, t : t + 1])
             h_pos.append(pos)
             h_neg.append(neg)
 
-        c_w = deal("c_w", gather("c_w_raw", x_word_win, cand_t, U32), U32, I32)
-        c_sc = deal("c_sc", gather("c_sc_raw", x_scale_win, cand_t, U8), U8, U8)
+        c_w_raw = gather("c_w_raw", x_word_win, cand_t, U32, "d_w_raw")
+        c_sc = deal("c_sc", c_sc_raw, U8, U8, 0, 2)
+        c_w = deal("c_w", c_w_raw, U32, I32, 0, 2)
 
         s_acc = [ps.tile([P, S], F32, name=f"s_acc{t}") for t in range(PACK)]
         s_t = [new(f"s_t{t}", [P, S], F32) for t in range(PACK)]
+        diffs = [new("diffs0", [P, 2, PACK, W], F32), new("diffs1", [P, 2, PACK, W], F32, "gains")]
+        pa = [d[:, 0, :, :] for d in diffs]
+        pb = [d[:, 1, :, :] for d in diffs]
+        pa16, pb16, above, below, raised = (
+            new(name, [P, S, PACK], BF16) for name in ("pa16", "pb16", "above", "below", "raised")
+        )
+        z16 = {lo: new(f"z16_{lo}", [P, PACK * (hi - lo)], BF16) for lo, hi in ((0, 256), (256, 384), (384, 512))}
+        z_w = new("z_w", [P, S], U32)
+        z_sc = new("z_sc", [P, S], U8)
 
-        def weave(name, planes, n):
-            woven = new(name, [P, n, PACK], BF16)
-            nc.scalar.copy(
-                woven[:].rearrange("p (c i) t -> p c t i", i=4),
-                planes[:].rearrange("p t (c i) -> p c t i", i=4),
+        def flat(tile, lo, hi):
+            return tile[:, lo:hi, :].rearrange("p n t -> p (n t)")
+
+        def weave(woven, planes, lo, hi, func):
+            first = lo // W * W
+            nc.scalar.activation(
+                woven[:, lo:hi, :].rearrange("p (c i) t -> p c t i", i=4),
+                planes[lo // W][:, :, lo - first : hi - first].rearrange("p t (c i) -> p c t i", i=4),
+                func,
             )
-            return woven[:].rearrange("p n t -> p (n t)")
 
-        def differences(c):
-            lo, hi = CHUNKS[c]
-            n = hi - lo
-            lists = slice(lo // 16, hi // 16)
-            pa = new(f"pa{c}", [P, PACK, n], F32)
-            pb = new(f"pb{c}", [P, PACK, n], F32)
+        def pa_plane(c, t):
+            lo, hi = HALVES[c]
+            window = h_neg[t][:].indirect(n1_t[:, lo // 16 : hi // 16])
+            nc.vector.tensor_tensor(pa[c][:, t, :], window, h_pos[t][:, lo:hi], ALU.add)
 
-            def pa_plane(t):
-                nc.vector.tensor_tensor(pa[:, t, :], h_neg[t][:].indirect(n1_t[:, lists]), h_pos[t][:, lo:hi], ALU.add)
+        def pb_plane(c, t):
+            lo, hi = HALVES[c]
+            window = h_pos[t][:].indirect(n2_t[:, lo // 16 : hi // 16])
+            nc.vector.tensor_tensor(pb[c][:, t, :], window, h_neg[t][:, lo:hi], ALU.add)
 
-            def pb_plane(t):
-                nc.vector.tensor_tensor(pb[:, t, :], h_pos[t][:].indirect(n2_t[:, lists]), h_neg[t][:, lo:hi], ALU.add)
+        def upper_bound(lo, hi):
+            nc.scalar.activation(flat(above, lo, hi), flat(pb16, lo, hi), ACT.Relu)
 
-            if c == 0:
-                for t in range(PACK):
-                    pb_plane(t)
-                    pa_plane(t)
-            else:
-                for t in range(PACK):
-                    pb_plane(t)
-                for t in range(PACK):
-                    pa_plane(t)
-            pb16 = weave(f"pb16_{c}", pb, n)
-            pa16 = weave(f"pa16_{c}", pa, n)
-            return pa16, pb16
+        def lower_bound(lo, hi):
+            nc.vector.tensor_scalar_min(flat(below, lo, hi), flat(pb16, lo, hi), 0.0)
 
-        def scores(c, pa16, pb16):
-            lo, hi = CHUNKS[c]
-            n = hi - lo
-            below = new(f"below{c}", [P, PACK * n], BF16)
-            above = new(f"above{c}", [P, PACK * n], BF16)
-            raised = new(f"raised{c}", [P, PACK * n], BF16)
-            z16 = new(f"z16_{c}", [P, PACK * n], BF16)
-            nc.vector.tensor_scalar_min(below[:], pb16, 0.0)
-            nc.vector.tensor_scalar_max(above[:], pb16, 0.0)
-            nc.vector.tensor_tensor(raised[:], pa16, below[:], ALU.max)
-            nc.vector.tensor_tensor(z16[:], raised[:], above[:], ALU.min)
-            z_w = new(f"z_w{c}", [P, n], U32)
-            z_sc = new(f"z_sc{c}", [P, n], U8)
-            nc.vector.quantize_mx(out=z_w[:].bitcast(FP8X4), scales=z_sc[:], in_=z16[:])
-            for t in range(PACK):
-                cols = slice(P * t, P * (t + 1))
-                nc.tensor.matmul_mx(
-                    out=s_acc[t][:, lo:hi], lhsT=c_w[:, cols].bitcast(FP8X4), lhsT_scale=c_sc[:, cols],
-                    rhs=z_w[:].bitcast(FP8X4), rhs_scale=z_sc[:], start=True, stop=True,
-                )
-                nc.scalar.mul(s_t[t][:, lo:hi], s_acc[t][:, lo:hi], 0.0625)
+        def clamp_below(lo, hi):
+            nc.vector.tensor_tensor(flat(raised, lo, hi), flat(pa16, lo, hi), flat(below, lo, hi), ALU.max)
 
-        pending = differences(0)
-        for c in range(1, len(CHUNKS)):
-            ahead = differences(c)
-            scores(c - 1, *pending)
-            pending = ahead
-        scores(len(CHUNKS) - 1, *pending)
+        def clamp_above(lo, hi):
+            nc.vector.tensor_tensor(z16[lo][:], flat(raised, lo, hi), flat(above, lo, hi), ALU.min)
+
+        def quantise_z(lo, hi):
+            nc.vector.quantize_mx(out=z_w[:, lo:hi].bitcast(FP8X4), scales=z_sc[:, lo:hi], in_=z16[lo][:])
+
+        def score(acc, words, scales, block, lo, hi):
+            cols = slice(P * block, P * (block + 1))
+            nc.tensor.matmul_mx(
+                out=acc, lhsT=words[:, cols].bitcast(FP8X4), lhsT_scale=scales[:, cols],
+                rhs=z_w[:, lo:hi].bitcast(FP8X4), rhs_scale=z_sc[:, lo:hi], start=True, stop=True,
+            )
+
+        def early_scores(lo, hi, banks):
+            for t in range(2):
+                score(banks[t][:, lo:hi], c_w, c_sc, t, lo, hi)
+                nc.scalar.mul(s_t[t][:, lo:hi], banks[t][:, lo:hi], 0.0625)
+
+        first, second = HALVES
+        third_q, fourth_q = (256, 384), (384, 512)
+        for t in range(PACK):
+            pb_plane(0, t)
+            pa_plane(0, t)
+        weave(pb16, pb, *first, ACT.Copy)
+        weave(pa16, pa, *first, ACT.Copy)
+        upper_bound(*first)
+        for t in range(PACK):
+            pb_plane(1, t)
+        weave(pb16, pb, *second, ACT.Copy)
+        pa_plane(1, 0)
+        pa_plane(1, 1)
+        lower_bound(*first)
+        pa_plane(1, 2)
+        clamp_below(*first)
+        pa_plane(1, 3)
+        weave(pa16, pa, *third_q, ACT.Copy)
+        weave(pa16, pa, *fourth_q, ACT.Copy)
+        clamp_above(*first)
+        lower_bound(*second)
+        nc.vector.tensor_scalar_max(flat(above, *second), flat(pb16, *second), 0.0)
+        quantise_z(*first)
+        early_scores(*first, s_acc)
+        for step in (clamp_below, clamp_above, quantise_z):
+            step(*third_q)
+            step(*fourth_q)
+        early_scores(*third_q, s_acc)
+        last_acc = [ps.tile([P, S], F32, name=f"last_acc{t}", tag=f"h_acc{t}") for t in range(2)]
+        early_scores(*fourth_q, last_acc)
+        late_sc = deal("late_sc", c_sc_raw, U8, U8, 2, 4, "z16_256")
+        late_w = deal("late_w", c_w_raw, U32, I32, 2, 4, "z16_384")
+        for t in range(2, PACK):
+            score(s_acc[t][:], late_w, late_sc, t - 2, 0, S)
 
         out_rows = out_0.rearrange("(p t) j -> t p j", t=PACK)
         woven = new("woven", [P, S, PACK], BF16)
-        gates = []
-        for t in range(PACK):
-            gate = new(f"gate{t}", [P, W], F32)
-            nc.scalar.activation(gate[:], s_t[t][:].indirect(n4_t[:]), ACT.Sigmoid)
-            gates.append(gate)
-        for t in range(PACK):
-            pa2 = new(f"pa2_{t}", [P, W], F32)
-            nc.vector.tensor_copy(pa2[:], s_t[t][:].indirect(n3_t[:]))
-            nc.vector.tensor_tensor(s_t[t][:].indirect(n4_t[:]), pa2[:], gates[t][:], ALU.mult)
+        gates = [new(f"gate{t}", [P, W], F32) for t in range(PACK)]
+        pa2 = [new(f"pa2_{t}", [P, W], F32) for t in range(PACK)]
+
+        def fetch(t):
+            if t >= 2:
+                nc.scalar.mul(s_t[t][:], s_acc[t][:], 0.0625)
+            nc.vector.tensor_copy(pa2[t][:], s_t[t][:].indirect(n3_t[:]))
+
+        def gate(t):
+            nc.scalar.activation(gates[t][:], s_t[t][:].indirect(n4_t[:]), ACT.Sigmoid)
+
+        def put_back(t):
+            nc.vector.tensor_tensor(s_t[t][:].indirect(n4_t[:]), pa2[t][:], gates[t][:], ALU.mult)
             nc.sync.dma_start(out_rows[t], s_t[t][:])
-            if t < 2:
-                nc.scalar.copy(woven[:, :, t], s_t[t][:])
-            elif t == 2:
-                nc.scalar.copy(woven[:, :, 2:4], s_t[t][:].unsqueeze(2).to_broadcast([P, S, 2]))
-            else:
-                for lo, hi in HALVES:
-                    nc.vector.tensor_copy(woven[:, lo:hi, t], s_t[t][:, lo:hi])
+
+        fetch(0)
+        for t in range(PACK):
+            if t + 1 < PACK:
+                fetch(t + 1)
+            gate(t)
+            put_back(t)
+        for t in range(2):
+            nc.scalar.copy(woven[:, :, t], s_t[t][:])
+        for lo, hi in (first, third_q):
+            nc.scalar.copy(woven[:, lo:hi, 2:4], s_t[2][:, lo:hi].unsqueeze(2).to_broadcast([P, hi - lo, 2]))
+        lo, hi = fourth_q
+        for t in (2, 3):
+            nc.scalar.copy(woven[:, lo:hi, t], s_t[t][:, lo:hi])
+        for lo, hi in (first, third_q):
+            nc.vector.tensor_copy(woven[:, lo:hi, 3], s_t[3][:, lo:hi])
 
         o_w = new("o_w", [P, S], U32)
         o_sc = new("o_sc", [P, S], U8)

@@ -17,7 +17,18 @@ ACT = mybir.ActivationFunctionType
 
 P = 128
 PACK = 4
-HALVES = ((0, 256), (256, 512))
+QUADRANT = 32
+BLOCKS = K // 32
+SPREAD = P // BLOCKS
+PICKS = 512
+LINE = 16
+SIXTEENTH = 0.0625
+
+HALF = S // 2
+FIRST, SECOND = (0, HALF), (HALF, S)
+HALVES = (FIRST, SECOND)
+THIRD_QUARTER, LAST_QUARTER = (HALF, 3 * S // 4), (3 * S // 4, S)
+EARLY = 2
 
 
 def tile_picked_pqcminmodfold_none_po_kernel(
@@ -25,232 +36,250 @@ def tile_picked_pqcminmodfold_none_po_kernel(
 ):
     nc = tc.nc
     with ExitStack() as ctx:
-        sb = ctx.enter_context(tc.tile_pool(name="sb", bufs=1))
-        ps = ctx.enter_context(tc.psum_pool(name="ps", bufs=1))
+        sbuf = ctx.enter_context(tc.tile_pool(name="sbuf", bufs=1))
+        psum = ctx.enter_context(tc.psum_pool(name="psum", bufs=1))
 
-        def new(name, shape, dtype, tag=None):
-            return sb.tile(shape, dtype, name=name, tag=tag or name, align_bytes=64)
+        def new(name, shape, dtype, after=None):
+            return sbuf.tile(shape, dtype, name=name, tag=after or name, align_bytes=64)
 
         def load_list(name, source):
             tile = new(name, [P, source.shape[1]], U16)
             nc.sync.dma_start(tile[:], source)
             return tile
 
-        def words_of(source):
-            return source[0].rearrange("p n t -> p (n t)").bitcast(I32)
+        def as_words(packed):
+            return packed[0].rearrange("p n t -> p (n t)").bitcast(I32)
 
-        d_scale_win = new("d_scale_win", [P, G], U8)
-        x_scale_win = new("x_scale_win", [P, T], U8)
-        nc.vector.memset(x_scale_win[:].bitcast(I32), 0)
-        for q in range(4):
+        d_scale_table = new("d_scale_table", [P, G], U8)
+        x_scale_table = new("x_scale_table", [P, T], U8)
+        nc.vector.memset(x_scale_table[:].bitcast(I32), 0)
+        for q in range(P // QUADRANT):
             nc.scalar.dma_start(
-                x_scale_win[32 * q : 32 * q + 4, :].bitcast(I32), x_scales[0][4 * q : 4 * q + 4, :].bitcast(I32)
+                x_scale_table[QUADRANT * q : QUADRANT * q + 4, :].bitcast(I32),
+                x_scales[0][4 * q : 4 * q + 4, :].bitcast(I32),
             )
 
-        k1_t = load_list("k1_t", k1)
+        k1_list = load_list("k1_list", k1)
         nc.sync.dma_start(
-            d_scale_win[:].bitcast(I32), d_scales[0].bitcast(I32).unsqueeze(1).to_broadcast([16, 8, G // 4])
+            d_scale_table[:].bitcast(I32),
+            d_scales[0].bitcast(I32).unsqueeze(1).to_broadcast([BLOCKS, SPREAD, G // 4]),
         )
-        offs_t = load_list("offs_t", offs)
-        x_word_win = new("x_word_win", [P, T], U32)
-        nc.sync.dma_start(x_word_win[:].bitcast(I32), words_of(x_words))
-        d_word_win = new("d_word_win", [P, G], U32)
-        nc.sync.dma_start(d_word_win[:].bitcast(I32), words_of(d_words))
-        cand_t = load_list("cand_t", cand)
-        gs_t = new("gs_t", [P, PACK], F32)
-        nc.sync.dma_start(gs_t[:], gs.rearrange("(p t) o -> p (t o)", t=PACK))
-        n1_t = load_list("n1_t", n1)
-        n2_t = load_list("n2_t", n2)
-        n3_t = load_list("n3_t", n3)
-        n4_t = load_list("n4_t", n4)
+        offs_list = load_list("offs_list", offs)
+        x_word_table = new("x_word_table", [P, T], U32)
+        nc.sync.dma_start(x_word_table[:].bitcast(I32), as_words(x_words))
+        d_word_table = new("d_word_table", [P, G], U32)
+        nc.sync.dma_start(d_word_table[:].bitcast(I32), as_words(d_words))
+        cand_list = load_list("cand_list", cand)
+        gs_planes = new("gs_planes", [P, PACK], F32)
+        nc.sync.dma_start(gs_planes[:], gs.rearrange("(p t) o -> p (t o)", t=PACK))
+        n1_list = load_list("n1_list", n1)
+        n2_list = load_list("n2_list", n2)
+        n3_list = load_list("n3_list", n3)
+        n4_list = load_list("n4_list", n4)
 
-        warm = new("warm", [P, PACK], F32)
-        nc.scalar.activation(warm[:], gs_t[:], ACT.Sigmoid)
+        warm_up = new("warm_up", [P, PACK], F32)
+        nc.scalar.activation(warm_up[:], gs_planes[:], ACT.Sigmoid)
         gains = new("gains", [P, 2, PACK], F32)
-        nc.scalar.mul(gains[:, 0, :], gs_t[:], 0.0625)
-        nc.scalar.mul(gains[:, 1, :], gs_t[:], -0.0625)
+        nc.scalar.mul(gains[:, 0, :], gs_planes[:], SIXTEENTH)
+        nc.scalar.mul(gains[:, 1, :], gs_planes[:], -SIXTEENTH)
 
-        def gather(name, window, offsets, dtype, tag=None):
-            picked = new(name, [P, 512], dtype, tag)
-            nc.vector.tensor_copy(picked[:], window[:].indirect(offsets[:]))
+        def gather(name, table, offsets, dtype, after=None):
+            picked = new(name, [P, PICKS], dtype, after)
+            nc.vector.tensor_copy(picked[:], table[:].indirect(offsets[:]))
             return picked
 
-        def deal(name, picked, dtype, view, t0=0, t1=PACK, tag=None):
-            dealt = new(name, [P, P * (t1 - t0)], dtype, tag)
-            run = 4 if dtype == U32 else 16
+        def deal(name, picked, view, run, planes, after=None):
+            dealt = new(name, [P, P * (planes.stop - planes.start)], picked.dtype, after)
             nc.vector.tensor_copy(
                 dealt[:].bitcast(view).rearrange("p (t c i) -> p c t i", i=run, c=P // run),
-                picked[:].bitcast(view).rearrange("p (c i t) -> p c t i", i=run, t=PACK)[:, :, t0:t1, :],
+                picked[:].bitcast(view).rearrange("p (c i t) -> p c t i", i=run, t=PACK)[:, :, planes, :],
             )
             return dealt
 
-        d_sc_raw = gather("d_sc_raw", d_scale_win, k1_t, U8)
-        xq_w = gather("xq_w", x_word_win, offs_t, U32)
-        d_sc = deal("d_sc", d_sc_raw, U8, U8)
+        def deal_words(name, picked, planes, after=None):
+            return deal(name, picked, I32, LINE // 4, planes, after)
+
+        def deal_scales(name, picked, planes, after=None):
+            return deal(name, picked, U8, LINE, planes, after)
+
+        all_planes, early_planes, late_planes = slice(0, PACK), slice(0, EARLY), slice(EARLY, PACK)
+
+        d_scales_picked = gather("d_scales_picked", d_scale_table, k1_list, U8)
+        token_words = gather("token_words", x_word_table, offs_list, U32)
+        d_scales_dealt = deal_scales("d_scales_dealt", d_scales_picked, all_planes)
         for r in range(1, 4):
-            nc.sync.dma_start(d_sc[r:P:32, :].bitcast(I32), d_sc[8 * r : P : 32, :].bitcast(I32))
-        xq_sc = gather("xq_sc", x_scale_win, offs_t, U8)
-        d_w_raw = gather("d_w_raw", d_word_win, k1_t, U32)
-        c_sc_raw = gather("c_sc_raw", x_scale_win, cand_t, U8, "d_word_win")
-        d_w = deal("d_w", d_w_raw, U32, I32)
+            nc.sync.dma_start(
+                d_scales_dealt[r:P:QUADRANT, :].bitcast(I32),
+                d_scales_dealt[SPREAD * r : P : QUADRANT, :].bitcast(I32),
+            )
+        token_scales = gather("token_scales", x_scale_table, offs_list, U8)
+        d_words_picked = gather("d_words_picked", d_word_table, k1_list, U32)
+        cand_scales_picked = gather("cand_scales_picked", x_scale_table, cand_list, U8, "d_word_table")
+        d_words_dealt = deal_words("d_words_dealt", d_words_picked, all_planes)
 
-        h_pos, h_neg = [], []
+        h_plus, h_minus = [], []
         for t in range(PACK):
-            cols = slice(P * t, P * (t + 1))
-            acc = ps.tile([P, S], F32, name=f"h_acc{t}", tag=f"h_acc{t}")
+            block = slice(P * t, P * (t + 1))
+            h_bank = psum.tile([P, S], F32, name=f"h_bank{t}", tag=f"h_bank{t}")
             nc.tensor.matmul_mx(
-                out=acc[:], lhsT=d_w[:, cols].bitcast(FP8X4), lhsT_scale=d_sc[:, cols],
-                rhs=xq_w[:].bitcast(FP8X4), rhs_scale=xq_sc[:], start=True, stop=True,
+                out=h_bank[:],
+                lhsT=d_words_dealt[:, block].bitcast(FP8X4),
+                lhsT_scale=d_scales_dealt[:, block],
+                rhs=token_words[:].bitcast(FP8X4),
+                rhs_scale=token_scales[:],
+                start=True,
+                stop=True,
             )
-            pos = new(f"h_pos{t}", [P, S], F32)
-            neg = new(f"h_neg{t}", [P, S], F32)
-            nc.scalar.activation(pos[:], acc[:], ACT.Copy, scale=gains[:, 0, t : t + 1])
-            nc.scalar.activation(neg[:], acc[:], ACT.Copy, scale=gains[:, 1, t : t + 1])
-            h_pos.append(pos)
-            h_neg.append(neg)
+            plus = new(f"h_plus{t}", [P, S], F32)
+            minus = new(f"h_minus{t}", [P, S], F32)
+            nc.scalar.activation(plus[:], h_bank[:], ACT.Copy, scale=gains[:, 0, t : t + 1])
+            nc.scalar.activation(minus[:], h_bank[:], ACT.Copy, scale=gains[:, 1, t : t + 1])
+            h_plus.append(plus)
+            h_minus.append(minus)
 
-        c_w_raw = gather("c_w_raw", x_word_win, cand_t, U32, "d_w_raw")
-        c_sc = deal("c_sc", c_sc_raw, U8, U8, 0, 2)
-        c_w = deal("c_w", c_w_raw, U32, I32, 0, 2)
+        cand_words_picked = gather("cand_words_picked", x_word_table, cand_list, U32, "d_words_picked")
+        early_scales = deal_scales("early_scales", cand_scales_picked, early_planes)
+        early_words = deal_words("early_words", cand_words_picked, early_planes)
 
-        s_acc = [ps.tile([P, S], F32, name=f"s_acc{t}") for t in range(PACK)]
-        s_t = [new(f"s_t{t}", [P, S], F32) for t in range(PACK)]
-        diffs = [new("diffs0", [P, 2, PACK, W], F32), new("diffs1", [P, 2, PACK, W], F32, "gains")]
-        pa = [d[:, 0, :, :] for d in diffs]
-        pb = [d[:, 1, :, :] for d in diffs]
-        pa16, pb16, above, below, raised = (
-            new(name, [P, S, PACK], BF16) for name in ("pa16", "pb16", "above", "below", "raised")
+        s_banks = [psum.tile([P, S], F32, name=f"s_bank{t}") for t in range(PACK)]
+        s_planes = [new(f"s_plane{t}", [P, S], F32) for t in range(PACK)]
+        differences = [
+            new("differences0", [P, 2, PACK, HALF], F32),
+            new("differences1", [P, 2, PACK, HALF], F32, "gains"),
+        ]
+        pa = [both[:, 0, :, :] for both in differences]
+        pb = [both[:, 1, :, :] for both in differences]
+        pa_woven, pb_woven, upper, lower, raised = (
+            new(name, [P, S, PACK], BF16) for name in ("pa_woven", "pb_woven", "upper", "lower", "raised")
         )
-        z16 = {lo: new(f"z16_{lo}", [P, PACK * (hi - lo)], BF16) for lo, hi in ((0, 256), (256, 384), (384, 512))}
-        z_w = new("z_w", [P, S], U32)
-        z_sc = new("z_sc", [P, S], U8)
+        z_woven = {
+            lo: new(f"z_woven{lo}", [P, PACK * (hi - lo)], BF16) for lo, hi in (FIRST, THIRD_QUARTER, LAST_QUARTER)
+        }
+        z_words = new("z_words", [P, S], U32)
+        z_scales = new("z_scales", [P, S], U8)
 
-        def flat(tile, lo, hi):
-            return tile[:, lo:hi, :].rearrange("p n t -> p (n t)")
+        def flat(woven, lo, hi):
+            return woven[:, lo:hi, :].rearrange("p n t -> p (n t)")
 
-        def weave(woven, planes, lo, hi, func):
-            first = lo // W * W
+        def weave(woven, halves, lo, hi):
+            base = lo // HALF * HALF
             nc.scalar.activation(
-                woven[:, lo:hi, :].rearrange("p (c i) t -> p c t i", i=4),
-                planes[lo // W][:, :, lo - first : hi - first].rearrange("p t (c i) -> p c t i", i=4),
-                func,
+                woven[:, lo:hi, :].rearrange("p (c i) t -> p c t i", i=LINE // 4),
+                halves[lo // HALF][:, :, lo - base : hi - base].rearrange("p t (c i) -> p c t i", i=LINE // 4),
+                ACT.Copy,
             )
 
-        def pa_plane(c, t):
-            lo, hi = HALVES[c]
-            window = h_neg[t][:].indirect(n1_t[:, lo // 16 : hi // 16])
-            nc.vector.tensor_tensor(pa[c][:, t, :], window, h_pos[t][:, lo:hi], ALU.add)
+        def make_pa(half, t):
+            lo, hi = HALVES[half]
+            looked_up = h_minus[t][:].indirect(n1_list[:, lo // 16 : hi // 16])
+            nc.vector.tensor_tensor(pa[half][:, t, :], looked_up, h_plus[t][:, lo:hi], ALU.add)
 
-        def pb_plane(c, t):
-            lo, hi = HALVES[c]
-            window = h_pos[t][:].indirect(n2_t[:, lo // 16 : hi // 16])
-            nc.vector.tensor_tensor(pb[c][:, t, :], window, h_neg[t][:, lo:hi], ALU.add)
+        def make_pb(half, t):
+            lo, hi = HALVES[half]
+            looked_up = h_plus[t][:].indirect(n2_list[:, lo // 16 : hi // 16])
+            nc.vector.tensor_tensor(pb[half][:, t, :], looked_up, h_minus[t][:, lo:hi], ALU.add)
 
-        def upper_bound(lo, hi):
-            nc.scalar.activation(flat(above, lo, hi), flat(pb16, lo, hi), ACT.Relu)
+        def make_bounds(lo, hi):
+            nc.vector.tensor_scalar_min(flat(lower, lo, hi), flat(pb_woven, lo, hi), 0.0)
+            nc.vector.tensor_scalar_max(flat(upper, lo, hi), flat(pb_woven, lo, hi), 0.0)
 
-        def lower_bound(lo, hi):
-            nc.vector.tensor_scalar_min(flat(below, lo, hi), flat(pb16, lo, hi), 0.0)
+        def clamp_from_below(lo, hi):
+            nc.vector.tensor_tensor(flat(raised, lo, hi), flat(pa_woven, lo, hi), flat(lower, lo, hi), ALU.max)
 
-        def clamp_below(lo, hi):
-            nc.vector.tensor_tensor(flat(raised, lo, hi), flat(pa16, lo, hi), flat(below, lo, hi), ALU.max)
-
-        def clamp_above(lo, hi):
-            nc.vector.tensor_tensor(z16[lo][:], flat(raised, lo, hi), flat(above, lo, hi), ALU.min)
+        def clamp_from_above(lo, hi):
+            nc.vector.tensor_tensor(z_woven[lo][:], flat(raised, lo, hi), flat(upper, lo, hi), ALU.min)
 
         def quantise_z(lo, hi):
-            nc.vector.quantize_mx(out=z_w[:, lo:hi].bitcast(FP8X4), scales=z_sc[:, lo:hi], in_=z16[lo][:])
-
-        def score(acc, words, scales, block, lo, hi):
-            cols = slice(P * block, P * (block + 1))
-            nc.tensor.matmul_mx(
-                out=acc, lhsT=words[:, cols].bitcast(FP8X4), lhsT_scale=scales[:, cols],
-                rhs=z_w[:, lo:hi].bitcast(FP8X4), rhs_scale=z_sc[:, lo:hi], start=True, stop=True,
+            nc.vector.quantize_mx(
+                out=z_words[:, lo:hi].bitcast(FP8X4), scales=z_scales[:, lo:hi], in_=z_woven[lo][:]
             )
 
-        def early_scores(lo, hi, banks):
-            for t in range(2):
-                score(banks[t][:, lo:hi], c_w, c_sc, t, lo, hi)
-                nc.scalar.mul(s_t[t][:, lo:hi], banks[t][:, lo:hi], 0.0625)
+        def multiply_z(out, words, scales, index, lo, hi):
+            block = slice(P * index, P * (index + 1))
+            nc.tensor.matmul_mx(
+                out=out,
+                lhsT=words[:, block].bitcast(FP8X4),
+                lhsT_scale=scales[:, block],
+                rhs=z_words[:, lo:hi].bitcast(FP8X4),
+                rhs_scale=z_scales[:, lo:hi],
+                start=True,
+                stop=True,
+            )
 
-        first, second = HALVES
-        third_q, fourth_q = (256, 384), (384, 512)
-        for t in range(PACK):
-            pb_plane(0, t)
-            pa_plane(0, t)
-        weave(pb16, pb, *first, ACT.Copy)
-        weave(pa16, pa, *first, ACT.Copy)
-        upper_bound(*first)
-        for t in range(PACK):
-            pb_plane(1, t)
-        weave(pb16, pb, *second, ACT.Copy)
-        pa_plane(1, 0)
-        pa_plane(1, 1)
-        lower_bound(*first)
-        pa_plane(1, 2)
-        clamp_below(*first)
-        pa_plane(1, 3)
-        weave(pa16, pa, *third_q, ACT.Copy)
-        weave(pa16, pa, *fourth_q, ACT.Copy)
-        clamp_above(*first)
-        lower_bound(*second)
-        nc.vector.tensor_scalar_max(flat(above, *second), flat(pb16, *second), 0.0)
-        quantise_z(*first)
-        early_scores(*first, s_acc)
-        for step in (clamp_below, clamp_above, quantise_z):
-            step(*third_q)
-            step(*fourth_q)
-        early_scores(*third_q, s_acc)
-        last_acc = [ps.tile([P, S], F32, name=f"last_acc{t}", tag=f"h_acc{t}") for t in range(2)]
-        early_scores(*fourth_q, last_acc)
-        late_sc = deal("late_sc", c_sc_raw, U8, U8, 2, 4, "z16_256")
-        late_w = deal("late_w", c_w_raw, U32, I32, 2, 4, "z16_384")
-        for t in range(2, PACK):
-            score(s_acc[t][:], late_w, late_sc, t - 2, 0, S)
+        def score_early_planes(lo, hi, banks):
+            for t in range(EARLY):
+                multiply_z(banks[t][:, lo:hi], early_words, early_scales, t, lo, hi)
+                nc.scalar.mul(s_planes[t][:, lo:hi], banks[t][:, lo:hi], SIXTEENTH)
 
-        out_rows = out_0.rearrange("(p t) j -> t p j", t=PACK)
-        woven = new("woven", [P, S, PACK], BF16)
+        for t in range(PACK):
+            make_pb(0, t)
+            make_pa(0, t)
+        weave(pb_woven, pb, *FIRST)
+        weave(pa_woven, pa, *FIRST)
+        for t in range(PACK):
+            make_pb(1, t)
+        weave(pb_woven, pb, *SECOND)
+        make_pa(1, 0)
+        make_pa(1, 1)
+        make_bounds(*FIRST)
+        make_pa(1, 2)
+        clamp_from_below(*FIRST)
+        make_pa(1, 3)
+        weave(pa_woven, pa, *THIRD_QUARTER)
+        weave(pa_woven, pa, *LAST_QUARTER)
+        clamp_from_above(*FIRST)
+        make_bounds(*SECOND)
+        quantise_z(*FIRST)
+        score_early_planes(*FIRST, s_banks)
+        for step in (clamp_from_below, clamp_from_above, quantise_z):
+            step(*THIRD_QUARTER)
+            step(*LAST_QUARTER)
+        score_early_planes(*THIRD_QUARTER, s_banks)
+        last_banks = [psum.tile([P, S], F32, name=f"last_bank{t}", tag=f"h_bank{t}") for t in range(EARLY)]
+        score_early_planes(*LAST_QUARTER, last_banks)
+        late_scales = deal_scales("late_scales", cand_scales_picked, late_planes, f"z_woven{THIRD_QUARTER[0]}")
+        late_words = deal_words("late_words", cand_words_picked, late_planes, f"z_woven{LAST_QUARTER[0]}")
+        for t in range(EARLY, PACK):
+            multiply_z(s_banks[t][:], late_words, late_scales, t - EARLY, 0, S)
+
+        out_planes = out_0.rearrange("(p t) j -> t p j", t=PACK)
+        out_woven = new("out_woven", [P, S, PACK], BF16)
         gates = [new(f"gate{t}", [P, W], F32) for t in range(PACK)]
         pa2 = [new(f"pa2_{t}", [P, W], F32) for t in range(PACK)]
 
-        def fetch(t):
-            if t >= 2:
-                nc.scalar.mul(s_t[t][:], s_acc[t][:], 0.0625)
-            nc.vector.tensor_copy(pa2[t][:], s_t[t][:].indirect(n3_t[:]))
+        def fetch_pa2(t):
+            if t >= EARLY:
+                nc.scalar.mul(s_planes[t][:], s_banks[t][:], SIXTEENTH)
+            nc.vector.tensor_copy(pa2[t][:], s_planes[t][:].indirect(n3_list[:]))
 
-        def gate(t):
-            nc.scalar.activation(gates[t][:], s_t[t][:].indirect(n4_t[:]), ACT.Sigmoid)
-
-        def put_back(t):
-            nc.vector.tensor_tensor(s_t[t][:].indirect(n4_t[:]), pa2[t][:], gates[t][:], ALU.mult)
-            nc.sync.dma_start(out_rows[t], s_t[t][:])
-
-        fetch(0)
+        fetch_pa2(0)
         for t in range(PACK):
             if t + 1 < PACK:
-                fetch(t + 1)
-            gate(t)
-            put_back(t)
-        for t in range(2):
-            nc.scalar.copy(woven[:, :, t], s_t[t][:])
-        for lo, hi in (first, third_q):
-            nc.scalar.copy(woven[:, lo:hi, 2:4], s_t[2][:, lo:hi].unsqueeze(2).to_broadcast([P, hi - lo, 2]))
-        lo, hi = fourth_q
-        for t in (2, 3):
-            nc.scalar.copy(woven[:, lo:hi, t], s_t[t][:, lo:hi])
-        for lo, hi in (first, third_q):
-            nc.vector.tensor_copy(woven[:, lo:hi, 3], s_t[3][:, lo:hi])
+                fetch_pa2(t + 1)
+            nc.scalar.activation(gates[t][:], s_planes[t][:].indirect(n4_list[:]), ACT.Sigmoid)
+            nc.vector.tensor_tensor(s_planes[t][:].indirect(n4_list[:]), pa2[t][:], gates[t][:], ALU.mult)
+            nc.sync.dma_start(out_planes[t], s_planes[t][:])
 
-        o_w = new("o_w", [P, S], U32)
-        o_sc = new("o_sc", [P, S], U8)
+        for t in (0, 1):
+            nc.scalar.copy(out_woven[:, :, t], s_planes[t][:])
+        for lo, hi in (FIRST, THIRD_QUARTER):
+            twice = s_planes[2][:, lo:hi].unsqueeze(2).to_broadcast([P, hi - lo, 2])
+            nc.scalar.copy(out_woven[:, lo:hi, 2:4], twice)
+        for t in (2, 3):
+            nc.scalar.copy(out_woven[:, slice(*LAST_QUARTER), t], s_planes[t][:, slice(*LAST_QUARTER)])
+        for lo, hi in (FIRST, THIRD_QUARTER):
+            nc.vector.tensor_copy(out_woven[:, lo:hi, 3], s_planes[3][:, lo:hi])
+
+        out_words = new("out_words", [P, S], U32)
+        out_scales = new("out_scales", [P, S], U8)
         for lo, hi in HALVES:
             nc.vector.quantize_mx(
-                out=o_w[:, lo:hi].bitcast(FP8X4), scales=o_sc[:, lo:hi],
-                in_=woven[:, lo:hi, :].rearrange("p n t -> p (n t)"),
+                out=out_words[:, lo:hi].bitcast(FP8X4), scales=out_scales[:, lo:hi], in_=flat(out_woven, lo, hi)
             )
-            nc.sync.dma_start(words_of(out_1)[:, lo:hi], o_w[:, lo:hi].bitcast(I32))
-        for q in range(4):
-            engine = nc.scalar if q % 2 else nc.sync
-            engine.dma_start(
-                out_2[0][4 * q : 4 * q + 4, :].bitcast(I32), o_sc[32 * q : 32 * q + 4, :].bitcast(I32)
+            nc.sync.dma_start(as_words(out_1)[:, lo:hi], out_words[:, lo:hi].bitcast(I32))
+        for q in range(P // QUADRANT):
+            queue = nc.scalar if q % 2 else nc.sync
+            queue.dma_start(
+                out_2[0][4 * q : 4 * q + 4, :].bitcast(I32),
+                out_scales[QUADRANT * q : QUADRANT * q + 4, :].bitcast(I32),
             )

from contextlib import ExitStack

import concourse.mybir as mybir

K, T, S, G, H, C, W = 512, 1024, 512, 2048, 512, 512, 256
FLOPS = 2 * K * H * S + 2 * K * C * S

F32 = mybir.dt.float32
BF16 = mybir.dt.bfloat16
I32 = mybir.dt.int32
U32 = mybir.dt.uint32
U16 = mybir.dt.uint16
U8 = mybir.dt.uint8
FP8X4 = mybir.dt.float8_e4m3fn_x4
ALU = mybir.AluOpType
ACT = mybir.ActivationFunctionType

P = 128
PACK = 4
QUADRANT = 32
BLOCKS = K // 32
SPREAD = P // BLOCKS
PICKS = 512
LINE = 16
SIXTEENTH = 0.0625

HALF = S // 2
FIRST, SECOND = (0, HALF), (HALF, S)
HALVES = (FIRST, SECOND)
THIRD_QUARTER, LAST_QUARTER = (HALF, 3 * S // 4), (3 * S // 4, S)
EARLY = 2


def tile_picked_pqcminmodfold_none_po_kernel(
    tc, x_words, x_scales, d_words, d_scales, gs, offs, k1, n1, n2, cand, n3, n4, out_0, out_1, out_2
):
    nc = tc.nc
    with ExitStack() as ctx:
        sbuf = ctx.enter_context(tc.tile_pool(name="sbuf", bufs=1))
        psum = ctx.enter_context(tc.psum_pool(name="psum", bufs=1))

        def new(name, shape, dtype, after=None):
            return sbuf.tile(shape, dtype, name=name, tag=after or name, align_bytes=64)

        def load_list(name, source):
            tile = new(name, [P, source.shape[1]], U16)
            nc.sync.dma_start(tile[:], source)
            return tile

        def as_words(packed):
            return packed[0].rearrange("p n t -> p (n t)").bitcast(I32)

        d_scale_table = new("d_scale_table", [P, G], U8)
        x_scale_table = new("x_scale_table", [P, T], U8)
        nc.vector.memset(x_scale_table[:].bitcast(I32), 0)
        for q in range(P // QUADRANT):
            nc.scalar.dma_start(
                x_scale_table[QUADRANT * q : QUADRANT * q + 4, :].bitcast(I32),
                x_scales[0][4 * q : 4 * q + 4, :].bitcast(I32),
            )

        k1_list = load_list("k1_list", k1)
        nc.sync.dma_start(
            d_scale_table[:].bitcast(I32),
            d_scales[0].bitcast(I32).unsqueeze(1).to_broadcast([BLOCKS, SPREAD, G // 4]),
        )
        offs_list = load_list("offs_list", offs)
        x_word_table = new("x_word_table", [P, T], U32)
        nc.sync.dma_start(x_word_table[:].bitcast(I32), as_words(x_words))
        d_word_table = new("d_word_table", [P, G], U32)
        nc.sync.dma_start(d_word_table[:].bitcast(I32), as_words(d_words))
        cand_list = load_list("cand_list", cand)
        gs_planes = new("gs_planes", [P, PACK], F32)
        nc.sync.dma_start(gs_planes[:], gs.rearrange("(p t) o -> p (t o)", t=PACK))
        n1_list = load_list("n1_list", n1)
        n2_list = load_list("n2_list", n2)
        n3_list = load_list("n3_list", n3)
        n4_list = load_list("n4_list", n4)

        warm_up = new("warm_up", [P, PACK], F32)
        nc.scalar.activation(warm_up[:], gs_planes[:], ACT.Sigmoid)
        gains = new("gains", [P, 2, PACK], F32)
        nc.scalar.mul(gains[:, 0, :], gs_planes[:], SIXTEENTH)
        nc.scalar.mul(gains[:, 1, :], gs_planes[:], -SIXTEENTH)

        def gather(name, table, offsets, dtype, after=None):
            picked = new(name, [P, PICKS], dtype, after)
            nc.vector.tensor_copy(picked[:], table[:].indirect(offsets[:]))
            return picked

        def deal(name, picked, view, run, planes, after=None):
            dealt = new(name, [P, P * (planes.stop - planes.start)], picked.dtype, after)
            nc.vector.tensor_copy(
                dealt[:].bitcast(view).rearrange("p (t c i) -> p c t i", i=run, c=P // run),
                picked[:].bitcast(view).rearrange("p (c i t) -> p c t i", i=run, t=PACK)[:, :, planes, :],
            )
            return dealt

        def deal_words(name, picked, planes, after=None):
            return deal(name, picked, I32, LINE // 4, planes, after)

        def deal_scales(name, picked, planes, after=None):
            return deal(name, picked, U8, LINE, planes, after)

        all_planes, early_planes, late_planes = slice(0, PACK), slice(0, EARLY), slice(EARLY, PACK)

        d_scales_picked = gather("d_scales_picked", d_scale_table, k1_list, U8)
        token_words = gather("token_words", x_word_table, offs_list, U32)
        d_scales_dealt = deal_scales("d_scales_dealt", d_scales_picked, all_planes)
        for r in range(1, 4):
            nc.sync.dma_start(
                d_scales_dealt[r:P:QUADRANT, :].bitcast(I32),
                d_scales_dealt[SPREAD * r : P : QUADRANT, :].bitcast(I32),
            )
        token_scales = gather("token_scales", x_scale_table, offs_list, U8)
        d_words_picked = gather("d_words_picked", d_word_table, k1_list, U32)
        cand_scales_picked = gather("cand_scales_picked", x_scale_table, cand_list, U8, "d_word_table")
        d_words_dealt = deal_words("d_words_dealt", d_words_picked, all_planes)

        h_plus, h_minus = [], []
        for t in range(PACK):
            block = slice(P * t, P * (t + 1))
            h_bank = psum.tile([P, S], F32, name=f"h_bank{t}", tag=f"h_bank{t}")
            nc.tensor.matmul_mx(
                out=h_bank[:],
                lhsT=d_words_dealt[:, block].bitcast(FP8X4),
                lhsT_scale=d_scales_dealt[:, block],
                rhs=token_words[:].bitcast(FP8X4),
                rhs_scale=token_scales[:],
                start=True,
                stop=True,
            )
            plus = new(f"h_plus{t}", [P, S], F32)
            minus = new(f"h_minus{t}", [P, S], F32)
            nc.scalar.activation(plus[:], h_bank[:], ACT.Copy, scale=gains[:, 0, t : t + 1])
            nc.scalar.activation(minus[:], h_bank[:], ACT.Copy, scale=gains[:, 1, t : t + 1])
            h_plus.append(plus)
            h_minus.append(minus)

        cand_words_picked = gather("cand_words_picked", x_word_table, cand_list, U32, "d_words_picked")
        early_scales = deal_scales("early_scales", cand_scales_picked, early_planes)
        early_words = deal_words("early_words", cand_words_picked, early_planes)

        s_banks = [psum.tile([P, S], F32, name=f"s_bank{t}") for t in range(PACK)]
        s_planes = [new(f"s_plane{t}", [P, S], F32) for t in range(PACK)]
        differences = [
            new("differences0", [P, 2, PACK, HALF], F32),
            new("differences1", [P, 2, PACK, HALF], F32, "gains"),
        ]
        pa = [both[:, 0, :, :] for both in differences]
        pb = [both[:, 1, :, :] for both in differences]
        pa_woven, pb_woven, upper, lower, raised = (
            new(name, [P, S, PACK], BF16) for name in ("pa_woven", "pb_woven", "upper", "lower", "raised")
        )
        z_woven = {
            lo: new(f"z_woven{lo}", [P, PACK * (hi - lo)], BF16) for lo, hi in (FIRST, THIRD_QUARTER, LAST_QUARTER)
        }
        z_words = new("z_words", [P, S], U32)
        z_scales = new("z_scales", [P, S], U8)

        def flat(woven, lo, hi):
            return woven[:, lo:hi, :].rearrange("p n t -> p (n t)")

        def weave(woven, halves, lo, hi):
            base = lo // HALF * HALF
            nc.scalar.activation(
                woven[:, lo:hi, :].rearrange("p (c i) t -> p c t i", i=LINE // 4),
                halves[lo // HALF][:, :, lo - base : hi - base].rearrange("p t (c i) -> p c t i", i=LINE // 4),
                ACT.Copy,
            )

        def make_pa(half, t):
            lo, hi = HALVES[half]
            looked_up = h_minus[t][:].indirect(n1_list[:, lo // 16 : hi // 16])
            nc.vector.tensor_tensor(pa[half][:, t, :], looked_up, h_plus[t][:, lo:hi], ALU.add)

        def make_pb(half, t):
            lo, hi = HALVES[half]
            looked_up = h_plus[t][:].indirect(n2_list[:, lo // 16 : hi // 16])
            nc.vector.tensor_tensor(pb[half][:, t, :], looked_up, h_minus[t][:, lo:hi], ALU.add)

        def make_bounds(lo, hi):
            nc.vector.tensor_scalar_min(flat(lower, lo, hi), flat(pb_woven, lo, hi), 0.0)
            nc.vector.tensor_scalar_max(flat(upper, lo, hi), flat(pb_woven, lo, hi), 0.0)

        def clamp_from_below(lo, hi):
            nc.vector.tensor_tensor(flat(raised, lo, hi), flat(pa_woven, lo, hi), flat(lower, lo, hi), ALU.max)

        def clamp_from_above(lo, hi):
            nc.vector.tensor_tensor(z_woven[lo][:], flat(raised, lo, hi), flat(upper, lo, hi), ALU.min)

        def quantise_z(lo, hi):
            nc.vector.quantize_mx(
                out=z_words[:, lo:hi].bitcast(FP8X4), scales=z_scales[:, lo:hi], in_=z_woven[lo][:]
            )

        def multiply_z(out, words, scales, index, lo, hi):
            block = slice(P * index, P * (index + 1))
            nc.tensor.matmul_mx(
                out=out,
                lhsT=words[:, block].bitcast(FP8X4),
                lhsT_scale=scales[:, block],
                rhs=z_words[:, lo:hi].bitcast(FP8X4),
                rhs_scale=z_scales[:, lo:hi],
                start=True,
                stop=True,
            )

        def score_early_planes(lo, hi, banks):
            for t in range(EARLY):
                multiply_z(banks[t][:, lo:hi], early_words, early_scales, t, lo, hi)
                nc.scalar.mul(s_planes[t][:, lo:hi], banks[t][:, lo:hi], SIXTEENTH)

        for t in range(PACK):
            make_pb(0, t)
            make_pa(0, t)
        weave(pb_woven, pb, *FIRST)
        weave(pa_woven, pa, *FIRST)
        for t in range(PACK):
            make_pb(1, t)
        weave(pb_woven, pb, *SECOND)
        make_pa(1, 0)
        make_pa(1, 1)
        make_bounds(*FIRST)
        make_pa(1, 2)
        clamp_from_below(*FIRST)
        make_pa(1, 3)
        weave(pa_woven, pa, *THIRD_QUARTER)
        weave(pa_woven, pa, *LAST_QUARTER)
        clamp_from_above(*FIRST)
        make_bounds(*SECOND)
        quantise_z(*FIRST)
        score_early_planes(*FIRST, s_banks)
        for step in (clamp_from_below, clamp_from_above, quantise_z):
            step(*THIRD_QUARTER)
            step(*LAST_QUARTER)
        score_early_planes(*THIRD_QUARTER, s_banks)
        last_banks = [psum.tile([P, S], F32, name=f"last_bank{t}", tag=f"h_bank{t}") for t in range(EARLY)]
        score_early_planes(*LAST_QUARTER, last_banks)
        late_scales = deal_scales("late_scales", cand_scales_picked, late_planes, f"z_woven{THIRD_QUARTER[0]}")
        late_words = deal_words("late_words", cand_words_picked, late_planes, f"z_woven{LAST_QUARTER[0]}")
        for t in range(EARLY, PACK):
            multiply_z(s_banks[t][:], late_words, late_scales, t - EARLY, 0, S)

        out_planes = out_0.rearrange("(p t) j -> t p j", t=PACK)
        out_woven = new("out_woven", [P, S, PACK], BF16)
        gates = [new(f"gate{t}", [P, W], F32) for t in range(PACK)]
        pa2 = [new(f"pa2_{t}", [P, W], F32) for t in range(PACK)]

        def fetch_pa2(t):
            if t >= EARLY:
                nc.scalar.mul(s_planes[t][:], s_banks[t][:], SIXTEENTH)
            nc.vector.tensor_copy(pa2[t][:], s_planes[t][:].indirect(n3_list[:]))

        fetch_pa2(0)
        for t in range(PACK):
            if t + 1 < PACK:
                fetch_pa2(t + 1)
            nc.scalar.activation(gates[t][:], s_planes[t][:].indirect(n4_list[:]), ACT.Sigmoid)
            nc.vector.tensor_tensor(s_planes[t][:].indirect(n4_list[:]), pa2[t][:], gates[t][:], ALU.mult)
            nc.sync.dma_start(out_planes[t], s_planes[t][:])

        for t in (0, 1):
            nc.scalar.copy(out_woven[:, :, t], s_planes[t][:])
        for lo, hi in (FIRST, THIRD_QUARTER):
            twice = s_planes[2][:, lo:hi].unsqueeze(2).to_broadcast([P, hi - lo, 2])
            nc.scalar.copy(out_woven[:, lo:hi, 2:4], twice)
        for t in (2, 3):
            nc.scalar.copy(out_woven[:, slice(*LAST_QUARTER), t], s_planes[t][:, slice(*LAST_QUARTER)])
        for lo, hi in (FIRST, THIRD_QUARTER):
            nc.vector.tensor_copy(out_woven[:, lo:hi, 3], s_planes[3][:, lo:hi])

        out_words = new("out_words", [P, S], U32)
        out_scales = new("out_scales", [P, S], U8)
        for lo, hi in HALVES:
            nc.vector.quantize_mx(
                out=out_words[:, lo:hi].bitcast(FP8X4), scales=out_scales[:, lo:hi], in_=flat(out_woven, lo, hi)
            )
            nc.sync.dma_start(as_words(out_1)[:, lo:hi], out_words[:, lo:hi].bitcast(I32))
        for q in range(P // QUADRANT):
            queue = nc.scalar if q % 2 else nc.sync
            queue.dma_start(
                out_2[0][4 * q : 4 * q + 4, :].bitcast(I32),
                out_scales[QUADRANT * q : QUADRANT * q + 4, :].bitcast(I32),
            )
